import numpy as np
import ml_dtypes


def mxq(x, axis, fmt="e4m3"):
    dtype, down = {"e4m3": (ml_dtypes.float8_e4m3fn, 7), "e5m2": (ml_dtypes.float8_e5m2, 14)}[fmt]
    v = np.moveaxis(np.asarray(x, np.float32).astype(ml_dtypes.bfloat16).astype(np.float64), axis, -1)
    blocks = v.reshape(v.shape[:-1] + (-1, 32))
    amax = np.abs(blocks).max(-1, keepdims=True)
    byte = np.maximum(np.where(amax > 0, np.frexp(amax)[1] - 1 + 127, 0) - down, 1)
    scale = np.exp2(byte - 127.0)
    codes = (blocks / scale).astype(np.float32).astype(dtype).astype(np.float64)
    return np.moveaxis((codes * scale).reshape(v.shape), -1, axis)


WIDE = False


def mx_kscale(k):
    if not WIDE:
        return np.ones(k)
    levels = np.array([10, -10, 5, -5, 0])
    if k % 512:
        return np.exp2(np.random.permutation(np.resize(levels, k // 32))).repeat(32)
    a = np.empty((k // 512, 16))
    for p in range(k // 512):
        a[p, :8] = np.random.permutation(np.resize(levels, 8))
        for g in range(8):
            far = levels[np.abs(levels - a[p, g]) >= 10]
            a[p, g + 8] = far[np.random.randint(len(far))]
    return np.exp2(a.ravel()).repeat(32)


def f64(x):
    return np.asarray(x).astype(np.float64)


def striped(idx):
    return np.tile(idx.reshape(-1, 16).T, (8, 1)).astype(np.uint16)


def unstriped(offs):
    return offs[:16].T.reshape(-1).astype(np.int64)


def pack_weight(w):
    k, n = w.shape
    w = f64(np.asarray(w, np.float32).astype(ml_dtypes.bfloat16)).reshape(k // 32, 32, n)
    amax = np.abs(w).max(1)
    byte = np.clip(np.where(amax > 0, np.frexp(amax)[1] - 1 + 127 - 7, 1), 1, 254)
    scaled = (w * np.exp2(127.0 - byte)[:, None, :]).reshape(k, n).astype(np.float32)
    words = np.ascontiguousarray(scaled.reshape(k // 512, 128, 4, n).transpose(0, 1, 3, 2)).astype(ml_dtypes.float8_e4m3fn).view(np.uint8)
    return words, np.ascontiguousarray(byte.astype(np.uint8).reshape(k // 512, 16, n))


def unpack_weight(words, scales):
    g, p, n, _ = words.shape
    vals = np.ascontiguousarray(words).view(ml_dtypes.float8_e4m3fn).astype(np.float64) * np.repeat(np.exp2(scales.astype(np.float64) - 127.0), 8, axis=1)[..., None]
    return vals.transpose(0, 1, 3, 2).reshape(g * 512, n)


E2M1 = np.array([0.0, 0.5, 1.0, 1.5, 2.0, 3.0, 4.0, 6.0, -0.0, -0.5, -1.0, -1.5, -2.0, -3.0, -4.0, -6.0])


def pack_fp4(w):
    k, n = w.shape
    w = f64(np.asarray(w, np.float32).astype(ml_dtypes.bfloat16)).reshape(k // 32, 32, n)
    amax = np.abs(w).max(1)
    mant, ex = np.frexp(amax / 6.0)
    byte = np.clip(np.where(amax > 0, np.where(mant > 0.5, ex, ex - 1) + 127, 1), 1, 254)
    scaled = (w * np.exp2(127.0 - byte)[:, None, :]).reshape(k, n).astype(np.float32)
    c = np.ascontiguousarray(scaled.reshape(k // 512, 128, 4, n).transpose(0, 1, 3, 2)).astype(ml_dtypes.float4_e2m1fn).view(np.uint8) & 0xF
    words = (c[..., 0::2] | (c[..., 1::2] << 4)).reshape(k // 512, 128, 2 * n)
    return np.ascontiguousarray(words), np.ascontiguousarray(byte.astype(np.uint8).reshape(k // 512, 16, n))


def unpack_fp4(words, scales):
    g, _, n = scales.shape
    words = np.ascontiguousarray(words).reshape(g, 128, n, 2)
    nib = np.empty((g, 128, n, 4), np.uint8)
    nib[..., 0::2] = words & 0xF
    nib[..., 1::2] = words >> 4
    vals = E2M1[nib] * np.repeat(np.exp2(scales.astype(np.float64) - 127.0), 8, axis=1)[..., None]
    return vals.transpose(0, 1, 3, 2).reshape(g * 512, n)


def planes(y):
    n, m = y.shape
    v = y.astype(np.float32).astype(ml_dtypes.bfloat16).astype(np.float64).reshape(n // 32, 32, m)
    top = np.abs(v).max(1)
    byte = np.clip(np.where(top > 0, np.frexp(top)[1] - 1 + 127 - 7, 1), 1, 254)
    codes = (v * np.exp2(127.0 - byte)[:, None, :]).reshape(n, m).astype(np.float32).astype(ml_dtypes.float8_e4m3fn).view(np.uint8)
    words = codes.reshape(n // 512, 128, 4, m).transpose(0, 1, 3, 2)
    return np.ascontiguousarray(words), np.ascontiguousarray(byte.astype(np.uint8).reshape(n // 512, 16, m))


K, T, S, N, H, U = 1024, 2048, 512, 512, 512, 1024


def setup_inputs():
    n = np.random.standard_normal
    s = mx_kscale(K)[:, None]
    u = mx_kscale(H)
    packed_xT = pack_weight(n((K, T)) * s)
    packed_w1 = pack_fp4(n((K, N)) / np.sqrt(K) / s)
    packed_w2 = pack_fp4(n((H, N)) / np.sqrt(H) / u[:, None])
    return {
        "x_words": packed_xT[0],
        "x_scales": packed_xT[1],
        "w1_words": packed_w1[0],
        "w1_scales": packed_w1[1],
        "unit": (np.random.uniform(0.6, 1.4, (H, 1)) * u[:, None]).astype(np.float32),
        "w2_words": packed_w2[0],
        "w2_scales": packed_w2[1],
        "offs": striped(np.random.permutation(T)[:S]),
        "ga": striped(np.random.permutation(np.concatenate([np.arange(S), np.random.randint(0, S, U - S)]))),
        "gb": striped(np.random.permutation(np.concatenate([np.arange(S), np.random.randint(0, S, U - S)]))),
        "gc": striped(np.random.permutation(np.concatenate([np.arange(S), np.random.randint(0, S, U - S)]))),
    }


def reference(x_words, x_scales, w1_words, w1_scales, unit, w2_words, w2_scales, offs, ga, gb, gc):
    xq = unpack_weight(x_words, x_scales)[:, unstriped(offs)]
    y = unpack_fp4(w1_words, w1_scales).T @ xq
    ya = y[:, unstriped(ga)]
    yb_ = y[:, unstriped(gb)]
    ygc = y[:, unstriped(gc)]
    tc = np.tanh(ygc)
    hid = f64(unit) * (ya * yb_ + tc * ya)
    out_0 = unpack_fp4(w2_words, w2_scales).T @ mxq(hid, 0, "e4m3")
    return (out_0,) + planes(out_0)

@@ -1,0 +1,208 @@
+from contextlib import ExitStack
+
+import concourse.mybir as mybir
+
+F32 = mybir.dt.float32
+BF16 = mybir.dt.bfloat16
+I32 = mybir.dt.int32
+U32 = mybir.dt.uint32
+U16 = mybir.dt.uint16
+U8 = mybir.dt.uint8
+FP8X4 = mybir.dt.float8_e4m3fn_x4
+FP4X4 = mybir.dt.float4_e2m1fn_x4
+ACT = mybir.ActivationFunctionType
+ALU = mybir.AluOpType
+
+P = 128
+PACK = 4
+PASSES = 2
+GENES = 2048
+PICKED = 512
+ROWS = 512
+TRIPLES = 1024
+BANK = 512
+CHUNKS = (256, 256, 256, 128, 128)
+VECTOR_EMPTIES = 3
+
+FLOPS = 2 * 1024 * ROWS * PICKED + 2 * ROWS * ROWS * TRIPLES
+
+
+def tile_picked_ytripco_mul_po_kernel(
+    tc, x_words, x_scales, w1_words, w1_scales, unit, w2_words, w2_scales, offs, ga, gb, gc, out_0, out_1, out_2
+):
+    nc = tc.nc
+    with ExitStack() as ctx:
+        keep = ctx.enter_context(tc.tile_pool(name="keep", bufs=1))
+        psum = ctx.enter_context(tc.psum_pool(name="psum", bufs=8))
+
+        def held(shape, dtype, name):
+            return keep.tile(shape, dtype, name=name, align_bytes=64)
+
+        def load_scale_rows(queue, plane, scales):
+            for q in range(4):
+                queue.dma_start(
+                    out=plane[32 * q : 32 * q + 4, :].bitcast(I32).rearrange("r (o c) -> r o c", o=scales.shape[0]),
+                    in_=scales[:, 4 * q : 4 * q + 4, :].bitcast(I32).rearrange("o r c -> r o c"),
+                )
+
+        def deal_words(engine, dealt, raw):
+            engine.tensor_copy(
+                out=dealt.rearrange("p (t m b) -> p t m b", t=PACK, b=2),
+                in_=raw.rearrange("p (m t b) -> p t m b", t=PACK, b=2),
+            )
+
+        def deal_scales(engine, dealt, raw):
+            engine.tensor_copy(
+                out=dealt.rearrange("p (t m) -> p t m", t=PACK),
+                in_=raw.rearrange("p (m t) -> p t m", t=PACK),
+            )
+
+        x_plane = keep.tile([P, PASSES * GENES], U8, name="x_plane", tag="plane_then_words", align_bytes=64)
+        nc.gpsimd.memset(x_plane[:].bitcast(I32), 0)
+        w_plane = held([P, PASSES * ROWS], U8, "w_plane")
+        nc.vector.memset(w_plane[:].bitcast(I32), 0)
+
+        offs_list = held([P, PICKED // 16], U16, "offs_list")
+        nc.sync.dma_start(offs_list[:], offs)
+        lists = {name: held([P, TRIPLES // 16], U16, f"list_{name}") for name in "abc"}
+        nc.sync.dma_start(lists["c"][:], gc)
+        nc.sync.dma_start(lists["b"][:], gb)
+        w_raw = held([P, PASSES * 2 * ROWS], U8, "w_raw")
+        nc.sync.dma_start(
+            out=w_raw[:].bitcast(I32).rearrange("p (o c) -> p o c", o=PASSES),
+            in_=w1_words.bitcast(I32).rearrange("o p c -> p o c"),
+        )
+        x_table = []
+        for o in range(PASSES):
+            table = held([P, GENES], I32, f"x_table{o}")
+            nc.sync.dma_start(out=table[:], in_=x_words[o].rearrange("p c r -> p (c r)").bitcast(I32))
+            x_table.append(table)
+        nc.sync.dma_start(lists["a"][:], ga)
+        load_scale_rows(nc.scalar, x_plane, x_scales)
+        load_scale_rows(nc.gpsimd, w_plane, w1_scales)
+        unit_cols = held([P, PACK], F32, "unit_cols")
+        nc.gpsimd.dma_start(out=unit_cols[:], in_=unit.rearrange("(p t) o -> p (t o)", t=PACK))
+
+        w1_dealt = [held([P, 2 * ROWS], U8, f"w1_dealt{o}") for o in range(PASSES)]
+        w1_plane = [held([P, ROWS], U8, f"w1_plane{o}") for o in range(PASSES)]
+        picked_plane = [held([P, PICKED], U8, f"picked_plane{o}") for o in range(PASSES)]
+        for o in range(PASSES):
+            deal_words(nc.vector, w1_dealt[o][:], w_raw[:, 2 * ROWS * o : 2 * ROWS * (o + 1)])
+        for o in range(PASSES):
+            nc.vector.tensor_copy(picked_plane[o][:], x_plane[:, o * GENES : (o + 1) * GENES].indirect(offs_list[:]))
+        for o in range(PASSES):
+            deal_scales(nc.gpsimd, w1_plane[o][:], w_plane[:, o * ROWS : (o + 1) * ROWS])
+        picked = [
+            keep.tile([P, PICKED], U32, name="picked0", tag="plane_then_words", align_bytes=64),
+            held([P, PICKED], U32, "picked1"),
+        ]
+        for o in range(PASSES):
+            nc.vector.tensor_copy(picked[o][:], x_table[o][:].bitcast(U32).indirect(offs_list[:]))
+
+        y_banks = [psum.tile([P, BANK], F32, name="bank") for t in range(PACK)]
+        for o in range(PASSES):
+            for t in range(PACK):
+                nc.tensor.matmul_mx(
+                    out=y_banks[t][:],
+                    lhsT=w1_dealt[o][:, 2 * P * t : 2 * P * (t + 1)].bitcast(FP4X4),
+                    lhsT_scale=w1_plane[o][:, P * t : P * (t + 1)],
+                    rhs=picked[o][:].bitcast(FP8X4),
+                    rhs_scale=picked_plane[o][:],
+                    start=(o == 0),
+                    stop=(o == PASSES - 1),
+                )
+
+        nc.sync.dma_start(out=w_raw[:, : 2 * ROWS].bitcast(I32), in_=w2_words[0].bitcast(I32))
+        load_scale_rows(nc.sync, w_plane[:, :ROWS], w2_scales)
+        w2_dealt = held([P, 2 * ROWS], U8, "w2_dealt")
+        w2_plane = held([P, ROWS], U8, "w2_plane")
+        deal_words(nc.gpsimd, w2_dealt[:], w_raw[:, : 2 * ROWS])
+        deal_scales(nc.gpsimd, w2_plane[:], w_plane[:, :ROWS])
+
+        y_plain = [held([P, PICKED], F32, f"y_plain{t}") for t in range(PACK)]
+        y_unit = [held([P, PICKED], F32, f"y_unit{t}") for t in range(PACK)]
+        y_tanh = [held([P, PICKED], F32, f"y_tanh{t}") for t in range(PACK)]
+        for t in range(PACK):
+            nc.scalar.activation(y_tanh[t][:], y_banks[t][:], ACT.Tanh)
+            nc.vector.tensor_copy(y_plain[t][:], y_banks[t][:])
+            nc.vector.tensor_scalar(y_unit[t][:], y_plain[t][:], unit_cols[:, t : t + 1], None, ALU.mult)
+
+        out_rows = out_0.rearrange("(p t) r -> p t r", t=PACK)
+        out_words = out_1[0].rearrange("p c r -> p (c r)").bitcast(I32)
+        out_plane = held([P, TRIPLES], U8, "out_plane")
+
+        def weave(flat):
+            return flat.rearrange("p (c i t) -> p c t i", i=4, t=PACK)
+
+        def rows(stack):
+            return stack.rearrange("p t (c i) -> p c t i", i=4)
+
+        def look_up(c, r0, n):
+            cols = slice(r0 // 16, (r0 + n) // 16)
+            third = held([P, PACK, n], F32, f"third{c}")
+            summed = held([P, PACK, n], F32, f"summed{c}")
+            first = held([P, PACK, n], F32, f"first{c}")
+            for t in range(PACK):
+                nc.scalar.activation(third[:, t, :], y_tanh[t][:].indirect(lists["c"][:, cols]), ACT.Copy)
+                nc.vector.tensor_tensor(
+                    summed[:, t, :], y_plain[t][:].indirect(lists["b"][:, cols]), third[:, t, :], ALU.add
+                )
+            return summed, first, cols
+
+        def look_up_first(first, cols, ts):
+            for t in ts:
+                nc.scalar.activation(first[:, t, :], y_unit[t][:].indirect(lists["a"][:, cols]), ACT.Copy)
+
+        def multiply(c, n, summed, first):
+            hid = held([P, PACK * n], BF16, f"hid{c}")
+            nc.vector.tensor_tensor(weave(hid[:]), rows(summed[:]), rows(first[:]), ALU.mult)
+            hid_words = held([P, n], U32, f"hid_words{c}")
+            hid_plane = held([P, n], U8, f"hid_plane{c}")
+            nc.vector.quantize_mx(out=hid_words[:].bitcast(FP8X4), scales=hid_plane[:], in_=hid[:])
+            per_bank = BANK // n
+            banks = []
+            for t in range(PACK):
+                if t % per_bank == 0:
+                    banks.append(psum.tile([P, BANK], F32, name="bank"))
+                nc.tensor.matmul_mx(
+                    out=banks[-1][:, (t % per_bank) * n : (t % per_bank + 1) * n],
+                    lhsT=w2_dealt[:, 2 * P * t : 2 * P * (t + 1)].bitcast(FP4X4),
+                    lhsT_scale=w2_plane[:, P * t : P * (t + 1)],
+                    rhs=hid_words[:].bitcast(FP8X4),
+                    rhs_scale=hid_plane[:],
+                    start=True,
+                    stop=True,
+                )
+            return banks
+
+        def hand_out(c, r0, n, banks):
+            result = held([P, PACK, n], F32, f"result{c}")
+            flat = result[:].rearrange("p t r -> p (t r)")
+            for b, bank in enumerate(banks):
+                if c < VECTOR_EMPTIES:
+                    nc.vector.tensor_copy(flat[:, b * BANK : (b + 1) * BANK], bank[:])
+                else:
+                    nc.scalar.copy(flat[:, b * BANK : (b + 1) * BANK], bank[:])
+            nc.sync.dma_start(out=out_rows[:, :, r0 : r0 + n], in_=result[:])
+            rounded = held([P, PACK * n], BF16, f"rounded{c}")
+            nc.vector.tensor_copy(weave(rounded[:]), rows(result[:]))
+            words = held([P, n], I32, f"words{c}")
+            nc.vector.quantize_mx(out=words[:].bitcast(FP8X4), scales=out_plane[:, r0 : r0 + n], in_=rounded[:])
+            nc.sync.dma_start(out=out_words[:, r0 : r0 + n], in_=words[:])
+
+        pending = None
+        r0 = 0
+        for c, n in enumerate(CHUNKS):
+            summed, first, cols = look_up(c, r0, n)
+            look_up_first(first, cols, (0,))
+            if pending is not None:
+                hand_out(*pending)
+            look_up_first(first, cols, (1, 2, 3))
+            pending = (c, r0, n, multiply(c, n, summed, first))
+            r0 += n
+        hand_out(*pending)
+        for q in range(4):
+            queue = nc.scalar if q % 2 == 0 else nc.sync
+            queue.dma_start(
+                out=out_2[0, 4 * q : 4 * q + 4, :].bitcast(I32), in_=out_plane[32 * q : 32 * q + 4, :].bitcast(I32)
+            )

@@ -57,19 +57,27 @@ def tile_picked_ytripco_mul_po_kernel(
                 in_=raw.rearrange("p (m t) -> p t m", t=PACK),
             )
 
-        x_plane = keep.tile([P, PASSES * GENES], U8, name="x_plane", tag="plane_then_words", align_bytes=64)
-        nc.gpsimd.memset(x_plane[:].bitcast(I32), 0)
-        w_plane = held([P, PASSES * ROWS], U8, "w_plane")
-        nc.vector.memset(w_plane[:].bitcast(I32), 0)
+        x_rows = held([P, GENES], U8, "x_rows")
+        nc.sync.dma_start(
+            out=x_rows[P - 32 :, :].bitcast(I32), in_=x_scales.rearrange("o q c -> (o q) c").bitcast(I32)
+        )
+        nc.vector.memset(x_rows[: P - 32, :].bitcast(I32), 0)
+        w1_rows = keep.tile([P, PASSES * ROWS], U8, name="w1_rows", tag="rows_then_words", align_bytes=64)
+        nc.gpsimd.memset(w1_rows[:].bitcast(I32), 0)
+        w2_rows = held([P, ROWS], U8, "w2_rows")
+        nc.vector.memset(w2_rows[:].bitcast(I32), 0)
+        picked_plane = held([P, PASSES * PICKED], U8, "picked_plane")
+        nc.vector.memset(picked_plane[:].bitcast(I32), 0)
 
         offs_list = held([P, PICKED // 16], U16, "offs_list")
         nc.sync.dma_start(offs_list[:], offs)
         lists = {name: held([P, TRIPLES // 16], U16, f"list_{name}") for name in "abc"}
         nc.sync.dma_start(lists["c"][:], gc)
         nc.sync.dma_start(lists["b"][:], gb)
-        w_raw = held([P, PASSES * 2 * ROWS], U8, "w_raw")
+        nc.sync.dma_start(lists["a"][:], ga)
+        w1_raw = held([P, PASSES * 2 * ROWS], U8, "w1_raw")
         nc.sync.dma_start(
-            out=w_raw[:].bitcast(I32).rearrange("p (o c) -> p o c", o=PASSES),
+            out=w1_raw[:].bitcast(I32).rearrange("p (o c) -> p o c", o=PASSES),
             in_=w1_words.bitcast(I32).rearrange("o p c -> p o c"),
         )
         x_table = []
@@ -77,24 +85,32 @@ def tile_picked_ytripco_mul_po_kernel(
             table = held([P, GENES], I32, f"x_table{o}")
             nc.sync.dma_start(out=table[:], in_=x_words[o].rearrange("p c r -> p (c r)").bitcast(I32))
             x_table.append(table)
-        nc.sync.dma_start(lists["a"][:], ga)
-        load_scale_rows(nc.scalar, x_plane, x_scales)
-        load_scale_rows(nc.gpsimd, w_plane, w1_scales)
+        load_scale_rows(nc.gpsimd, w1_rows, w1_scales)
+
+        picked_rows = held([P, PICKED], U8, "picked_rows")
+        nc.vector.tensor_copy(picked_rows[:], x_rows[:].indirect(offs_list[:]))
+        for o in range(PASSES):
+            for q in range(4):
+                queue = nc.gpsimd if (o, q) == (PASSES - 1, 3) else nc.scalar
+                row = P - 32 + 16 * o + 4 * q
+                queue.dma_start(
+                    out=picked_plane[32 * q : 32 * q + 4, o * PICKED : (o + 1) * PICKED].bitcast(I32),
+                    in_=picked_rows[row : row + 4, :].bitcast(I32),
+                )
         unit_cols = held([P, PACK], F32, "unit_cols")
         nc.gpsimd.dma_start(out=unit_cols[:], in_=unit.rearrange("(p t) o -> p (t o)", t=PACK))
-
+        w2_raw = held([P, 2 * ROWS], U8, "w2_raw")
+        nc.gpsimd.dma_start(out=w2_raw[:].bitcast(I32), in_=w2_words[0].bitcast(I32))
+        load_scale_rows(nc.gpsimd, w2_rows, w2_scales)
         w1_dealt = [held([P, 2 * ROWS], U8, f"w1_dealt{o}") for o in range(PASSES)]
         w1_plane = [held([P, ROWS], U8, f"w1_plane{o}") for o in range(PASSES)]
-        picked_plane = [held([P, PICKED], U8, f"picked_plane{o}") for o in range(PASSES)]
         for o in range(PASSES):
-            deal_words(nc.vector, w1_dealt[o][:], w_raw[:, 2 * ROWS * o : 2 * ROWS * (o + 1)])
+            deal_words(nc.vector, w1_dealt[o][:], w1_raw[:, 2 * ROWS * o : 2 * ROWS * (o + 1)])
         for o in range(PASSES):
-            nc.vector.tensor_copy(picked_plane[o][:], x_plane[:, o * GENES : (o + 1) * GENES].indirect(offs_list[:]))
-        for o in range(PASSES):
-            deal_scales(nc.gpsimd, w1_plane[o][:], w_plane[:, o * ROWS : (o + 1) * ROWS])
+            deal_scales(nc.vector, w1_plane[o][:], w1_rows[:, o * ROWS : (o + 1) * ROWS])
         picked = [
-            keep.tile([P, PICKED], U32, name="picked0", tag="plane_then_words", align_bytes=64),
-            held([P, PICKED], U32, "picked1"),
+            held([P, PICKED], U32, "picked0"),
+            keep.tile([P, PICKED], U32, name="picked1", tag="rows_then_words", align_bytes=64),
         ]
         for o in range(PASSES):
             nc.vector.tensor_copy(picked[o][:], x_table[o][:].bitcast(U32).indirect(offs_list[:]))
@@ -107,17 +123,14 @@ def tile_picked_ytripco_mul_po_kernel(
                     lhsT=w1_dealt[o][:, 2 * P * t : 2 * P * (t + 1)].bitcast(FP4X4),
                     lhsT_scale=w1_plane[o][:, P * t : P * (t + 1)],
                     rhs=picked[o][:].bitcast(FP8X4),
-                    rhs_scale=picked_plane[o][:],
+                    rhs_scale=picked_plane[:, o * PICKED : (o + 1) * PICKED],
                     start=(o == 0),
                     stop=(o == PASSES - 1),
                 )
 
-        nc.sync.dma_start(out=w_raw[:, : 2 * ROWS].bitcast(I32), in_=w2_words[0].bitcast(I32))
-        load_scale_rows(nc.sync, w_plane[:, :ROWS], w2_scales)
         w2_dealt = held([P, 2 * ROWS], U8, "w2_dealt")
         w2_plane = held([P, ROWS], U8, "w2_plane")
-        deal_words(nc.gpsimd, w2_dealt[:], w_raw[:, : 2 * ROWS])
-        deal_scales(nc.gpsimd, w2_plane[:], w_plane[:, :ROWS])
+        deal_words(nc.vector, w2_dealt[:], w2_raw[:])
 
         y_plain = [held([P, PICKED], F32, f"y_plain{t}") for t in range(PACK)]
         y_unit = [held([P, PICKED], F32, f"y_unit{t}") for t in range(PACK)]
@@ -126,6 +139,7 @@ def tile_picked_ytripco_mul_po_kernel(
             nc.scalar.activation(y_tanh[t][:], y_banks[t][:], ACT.Tanh)
             nc.vector.tensor_copy(y_plain[t][:], y_banks[t][:])
             nc.vector.tensor_scalar(y_unit[t][:], y_plain[t][:], unit_cols[:, t : t + 1], None, ALU.mult)
+        deal_scales(nc.vector, w2_plane[:], w2_rows[:])
 
         out_rows = out_0.rearrange("(p t) r -> p t r", t=PACK)
         out_words = out_1[0].rearrange("p c r -> p (c r)").bitcast(I32)
@@ -179,7 +193,7 @@ def tile_picked_ytripco_mul_po_kernel(
             result = held([P, PACK, n], F32, f"result{c}")
             flat = result[:].rearrange("p t r -> p (t r)")
             for b, bank in enumerate(banks):
-                if c < VECTOR_EMPTIES:
+                if PACK * r0 // BANK + b < VECTOR_EMPTIES:
                     nc.vector.tensor_copy(flat[:, b * BANK : (b + 1) * BANK], bank[:])
                 else:
                     nc.scalar.copy(flat[:, b * BANK : (b + 1) * BANK], bank[:])

@@ -22,7 +22,7 @@ ROWS = 512
 TRIPLES = 1024
 BANK = 512
 CHUNKS = (256, 256, 256, 128, 128)
-VECTOR_EMPTIES = 3
+VECTOR_EMPTIES = 1
 
 FLOPS = 2 * 1024 * ROWS * PICKED + 2 * ROWS * ROWS * TRIPLES
 
@@ -37,6 +37,9 @@ def tile_picked_ytripco_mul_po_kernel(
 
         def held(shape, dtype, name):
             return keep.tile(shape, dtype, name=name, align_bytes=64)
+
+        def shared(shape, dtype, name, tag):
+            return keep.tile(shape, dtype, name=name, tag=tag, align_bytes=64)
 
         def load_scale_rows(queue, plane, scales):
             for q in range(4):
@@ -62,10 +65,8 @@ def tile_picked_ytripco_mul_po_kernel(
             out=x_rows[P - 32 :, :].bitcast(I32), in_=x_scales.rearrange("o q c -> (o q) c").bitcast(I32)
         )
         nc.vector.memset(x_rows[: P - 32, :].bitcast(I32), 0)
-        w1_rows = keep.tile([P, PASSES * ROWS], U8, name="w1_rows", tag="rows_then_words", align_bytes=64)
+        w1_rows = shared([P, PASSES * ROWS], U8, "w1_rows", "w1_rows_picked1")
         nc.gpsimd.memset(w1_rows[:].bitcast(I32), 0)
-        w2_rows = held([P, ROWS], U8, "w2_rows")
-        nc.vector.memset(w2_rows[:].bitcast(I32), 0)
         picked_plane = held([P, PASSES * PICKED], U8, "picked_plane")
         nc.vector.memset(picked_plane[:].bitcast(I32), 0)
 
@@ -75,19 +76,19 @@ def tile_picked_ytripco_mul_po_kernel(
         nc.sync.dma_start(lists["c"][:], gc)
         nc.sync.dma_start(lists["b"][:], gb)
         nc.sync.dma_start(lists["a"][:], ga)
-        w1_raw = held([P, PASSES * 2 * ROWS], U8, "w1_raw")
+        w1_raw = shared([P, PASSES * 2 * ROWS], U8, "w1_raw", "w1_raw_unit")
         nc.sync.dma_start(
             out=w1_raw[:].bitcast(I32).rearrange("p (o c) -> p o c", o=PASSES),
             in_=w1_words.bitcast(I32).rearrange("o p c -> p o c"),
         )
         x_table = []
         for o in range(PASSES):
-            table = held([P, GENES], I32, f"x_table{o}")
+            table = shared([P, GENES], I32, f"x_table{o}", f"x_table{o}")
             nc.sync.dma_start(out=table[:], in_=x_words[o].rearrange("p c r -> p (c r)").bitcast(I32))
             x_table.append(table)
         load_scale_rows(nc.gpsimd, w1_rows, w1_scales)
 
-        picked_rows = held([P, PICKED], U8, "picked_rows")
+        picked_rows = shared([P, PICKED], U8, "picked_rows", "picked_rows_w2_raw")
         nc.vector.tensor_copy(picked_rows[:], x_rows[:].indirect(offs_list[:]))
         for o in range(PASSES):
             for q in range(4):
@@ -97,23 +98,16 @@ def tile_picked_ytripco_mul_po_kernel(
                     out=picked_plane[32 * q : 32 * q + 4, o * PICKED : (o + 1) * PICKED].bitcast(I32),
                     in_=picked_rows[row : row + 4, :].bitcast(I32),
                 )
-        unit_cols = held([P, PACK], F32, "unit_cols")
-        nc.gpsimd.dma_start(out=unit_cols[:], in_=unit.rearrange("(p t) o -> p (t o)", t=PACK))
-        w2_raw = held([P, 2 * ROWS], U8, "w2_raw")
-        nc.gpsimd.dma_start(out=w2_raw[:].bitcast(I32), in_=w2_words[0].bitcast(I32))
-        load_scale_rows(nc.gpsimd, w2_rows, w2_scales)
         w1_dealt = [held([P, 2 * ROWS], U8, f"w1_dealt{o}") for o in range(PASSES)]
-        w1_plane = [held([P, ROWS], U8, f"w1_plane{o}") for o in range(PASSES)]
         for o in range(PASSES):
             deal_words(nc.vector, w1_dealt[o][:], w1_raw[:, 2 * ROWS * o : 2 * ROWS * (o + 1)])
+        picked = [held([P, PICKED], U32, "picked0")]
+        nc.vector.tensor_copy(picked[0][:], x_table[0][:].bitcast(U32).indirect(offs_list[:]))
+        w1_plane = [shared([P, ROWS], U8, "w1_plane0", "x_table0"), held([P, ROWS], U8, "w1_plane1")]
         for o in range(PASSES):
             deal_scales(nc.vector, w1_plane[o][:], w1_rows[:, o * ROWS : (o + 1) * ROWS])
-        picked = [
-            held([P, PICKED], U32, "picked0"),
-            keep.tile([P, PICKED], U32, name="picked1", tag="rows_then_words", align_bytes=64),
-        ]
-        for o in range(PASSES):
-            nc.vector.tensor_copy(picked[o][:], x_table[o][:].bitcast(U32).indirect(offs_list[:]))
+        picked.append(shared([P, PICKED], U32, "picked1", "w1_rows_picked1"))
+        nc.vector.tensor_copy(picked[1][:], x_table[1][:].bitcast(U32).indirect(offs_list[:]))
 
         y_banks = [psum.tile([P, BANK], F32, name="bank") for t in range(PACK)]
         for o in range(PASSES):
@@ -128,17 +122,22 @@ def tile_picked_ytripco_mul_po_kernel(
                     stop=(o == PASSES - 1),
                 )
 
+        unit_cols = shared([P, PACK], F32, "unit_cols", "w1_raw_unit")
+        nc.sync.dma_start(out=unit_cols[:], in_=unit.rearrange("(p t) o -> p (t o)", t=PACK))
+        w2_raw = shared([P, 2 * ROWS], U8, "w2_raw", "picked_rows_w2_raw")
+        nc.sync.dma_start(out=w2_raw[:].bitcast(I32), in_=w2_words[0].bitcast(I32))
+        w2_rows = shared([P, ROWS], U8, "w2_rows", "x_table1")
+        nc.gpsimd.memset(w2_rows[:].bitcast(I32), 0)
+        load_scale_rows(nc.sync, w2_rows, w2_scales)
         w2_dealt = held([P, 2 * ROWS], U8, "w2_dealt")
         w2_plane = held([P, ROWS], U8, "w2_plane")
         deal_words(nc.vector, w2_dealt[:], w2_raw[:])
 
         y_plain = [held([P, PICKED], F32, f"y_plain{t}") for t in range(PACK)]
-        y_unit = [held([P, PICKED], F32, f"y_unit{t}") for t in range(PACK)]
         y_tanh = [held([P, PICKED], F32, f"y_tanh{t}") for t in range(PACK)]
         for t in range(PACK):
             nc.scalar.activation(y_tanh[t][:], y_banks[t][:], ACT.Tanh)
             nc.vector.tensor_copy(y_plain[t][:], y_banks[t][:])
-            nc.vector.tensor_scalar(y_unit[t][:], y_plain[t][:], unit_cols[:, t : t + 1], None, ALU.mult)
         deal_scales(nc.vector, w2_plane[:], w2_rows[:])
 
         out_rows = out_0.rearrange("(p t) r -> p t r", t=PACK)
@@ -165,11 +164,16 @@ def tile_picked_ytripco_mul_po_kernel(
 
         def look_up_first(first, cols, ts):
             for t in ts:
-                nc.scalar.activation(first[:, t, :], y_unit[t][:].indirect(lists["a"][:, cols]), ACT.Copy)
+                nc.scalar.activation(first[:, t, :], y_plain[t][:].indirect(lists["a"][:, cols]), ACT.Copy)
 
         def multiply(c, n, summed, first):
             hid = held([P, PACK * n], BF16, f"hid{c}")
-            nc.vector.tensor_tensor(weave(hid[:]), rows(summed[:]), rows(first[:]), ALU.mult)
+            exact = held([P, PACK, n], F32, f"exact{c}")
+            for t in range(PACK):
+                nc.vector.scalar_tensor_tensor(
+                    exact[:, t, :], first[:, t, :], unit_cols[:, t : t + 1], summed[:, t, :], ALU.mult, ALU.mult
+                )
+            nc.vector.tensor_copy(weave(hid[:]), rows(exact[:]))
             hid_words = held([P, n], U32, f"hid_words{c}")
             hid_plane = held([P, n], U8, f"hid_plane{c}")
             nc.vector.quantize_mx(out=hid_words[:].bitcast(FP8X4), scales=hid_plane[:], in_=hid[:])

@@ -15,16 +15,25 @@ ALU = mybir.AluOpType
 
 P = 128
 PACK = 4
+QUADS = 4
+QUAD = 32
+LIVE = 4
 PASSES = 2
 GENES = 2048
 PICKED = 512
 ROWS = 512
 TRIPLES = 1024
+PER_COLUMN = 16
+FP4_BYTES = 2
 BANK = 512
-CHUNKS = (256, 256, 256, 128, 128)
-VECTOR_EMPTIES = 1
+BANKS = 8
+LINE = 4
+WIDTHS = (128, 256, 512)
 
-FLOPS = 2 * 1024 * ROWS * PICKED + 2 * ROWS * ROWS * TRIPLES
+CHUNKS = (384, 256, 256, 128)
+GA_ON_VECTOR = (1, 2, 1, 1)
+
+FLOPS = 2 * PASSES * PACK * P * ROWS * PICKED + 2 * ROWS * ROWS * TRIPLES
 
 
 def tile_picked_ytripco_mul_po_kernel(
@@ -33,7 +42,7 @@ def tile_picked_ytripco_mul_po_kernel(
     nc = tc.nc
     with ExitStack() as ctx:
         keep = ctx.enter_context(tc.tile_pool(name="keep", bufs=1))
-        psum = ctx.enter_context(tc.psum_pool(name="psum", bufs=8))
+        psum = ctx.enter_context(tc.psum_pool(name="psum", bufs=BANKS))
 
         def held(shape, dtype, name):
             return keep.tile(shape, dtype, name=name, align_bytes=64)
@@ -42,41 +51,43 @@ def tile_picked_ytripco_mul_po_kernel(
             return keep.tile(shape, dtype, name=name, tag=tag, align_bytes=64)
 
         def load_scale_rows(queue, plane, scales):
-            for q in range(4):
+            for q in range(QUADS):
                 queue.dma_start(
-                    out=plane[32 * q : 32 * q + 4, :].bitcast(I32).rearrange("r (o c) -> r o c", o=scales.shape[0]),
-                    in_=scales[:, 4 * q : 4 * q + 4, :].bitcast(I32).rearrange("o r c -> r o c"),
+                    out=plane[QUAD * q : QUAD * q + LIVE, :]
+                    .bitcast(I32)
+                    .rearrange("r (o c) -> r o c", o=scales.shape[0]),
+                    in_=scales[:, LIVE * q : LIVE * (q + 1), :].bitcast(I32).rearrange("o r c -> r o c"),
                 )
 
-        def deal_words(engine, dealt, raw):
-            engine.tensor_copy(
-                out=dealt.rearrange("p (t m b) -> p t m b", t=PACK, b=2),
-                in_=raw.rearrange("p (m t b) -> p t m b", t=PACK, b=2),
+        def deal_words(dealt, raw):
+            nc.vector.tensor_copy(
+                out=dealt.rearrange("p (t m b) -> p t m b", t=PACK, b=FP4_BYTES),
+                in_=raw.rearrange("p (m t b) -> p t m b", t=PACK, b=FP4_BYTES),
             )
 
-        def deal_scales(engine, dealt, raw):
-            engine.tensor_copy(
-                out=dealt.rearrange("p (t m) -> p t m", t=PACK),
-                in_=raw.rearrange("p (m t) -> p t m", t=PACK),
-            )
+        def fp4_columns(dealt, t):
+            return dealt[:, FP4_BYTES * P * t : FP4_BYTES * P * (t + 1)].bitcast(FP4X4)
 
-        x_rows = held([P, GENES], U8, "x_rows")
+        rows_start = P - PASSES * QUADS * LIVE
+        x_rows = shared([P, GENES], U8, "x_rows", "x_rows_unit")
         nc.sync.dma_start(
-            out=x_rows[P - 32 :, :].bitcast(I32), in_=x_scales.rearrange("o q c -> (o q) c").bitcast(I32)
+            out=x_rows[rows_start:, :].bitcast(I32), in_=x_scales.rearrange("o q c -> (o q) c").bitcast(I32)
         )
-        nc.vector.memset(x_rows[: P - 32, :].bitcast(I32), 0)
-        w1_rows = shared([P, PASSES * ROWS], U8, "w1_rows", "w1_rows_picked1")
+        nc.vector.memset(x_rows[:rows_start, :].bitcast(I32), 0)
+        w1_rows = held([P, PASSES * ROWS], U8, "w1_rows")
         nc.gpsimd.memset(w1_rows[:].bitcast(I32), 0)
         picked_plane = held([P, PASSES * PICKED], U8, "picked_plane")
         nc.vector.memset(picked_plane[:].bitcast(I32), 0)
 
-        offs_list = held([P, PICKED // 16], U16, "offs_list")
+        offs_list = held([P, PICKED // PER_COLUMN], U16, "offs_list")
         nc.sync.dma_start(offs_list[:], offs)
-        lists = {name: held([P, TRIPLES // 16], U16, f"list_{name}") for name in "abc"}
-        nc.sync.dma_start(lists["c"][:], gc)
-        nc.sync.dma_start(lists["b"][:], gb)
-        nc.sync.dma_start(lists["a"][:], ga)
-        w1_raw = shared([P, PASSES * 2 * ROWS], U8, "w1_raw", "w1_raw_unit")
+        ga_list = held([P, TRIPLES // PER_COLUMN], U16, "ga_list")
+        gb_list = held([P, TRIPLES // PER_COLUMN], U16, "gb_list")
+        gc_list = held([P, TRIPLES // PER_COLUMN], U16, "gc_list")
+        nc.sync.dma_start(gc_list[:], gc)
+        nc.sync.dma_start(gb_list[:], gb)
+        nc.sync.dma_start(ga_list[:], ga)
+        w1_raw = shared([P, PASSES * FP4_BYTES * ROWS], U8, "w1_raw", "w1_raw_w2_rows")
         nc.sync.dma_start(
             out=w1_raw[:].bitcast(I32).rearrange("p (o c) -> p o c", o=PASSES),
             in_=w1_words.bitcast(I32).rearrange("o p c -> p o c"),
@@ -91,119 +102,125 @@ def tile_picked_ytripco_mul_po_kernel(
         picked_rows = shared([P, PICKED], U8, "picked_rows", "picked_rows_w2_raw")
         nc.vector.tensor_copy(picked_rows[:], x_rows[:].indirect(offs_list[:]))
         for o in range(PASSES):
-            for q in range(4):
-                queue = nc.gpsimd if (o, q) == (PASSES - 1, 3) else nc.scalar
-                row = P - 32 + 16 * o + 4 * q
+            for q in range(QUADS):
+                queue = nc.gpsimd if (o, q) == (PASSES - 1, QUADS - 1) else nc.scalar
+                row = rows_start + LIVE * (QUADS * o + q)
                 queue.dma_start(
-                    out=picked_plane[32 * q : 32 * q + 4, o * PICKED : (o + 1) * PICKED].bitcast(I32),
-                    in_=picked_rows[row : row + 4, :].bitcast(I32),
+                    out=picked_plane[QUAD * q : QUAD * q + LIVE, o * PICKED : (o + 1) * PICKED].bitcast(I32),
+                    in_=picked_rows[row : row + LIVE, :].bitcast(I32),
                 )
-        w1_dealt = [held([P, 2 * ROWS], U8, f"w1_dealt{o}") for o in range(PASSES)]
+        w1_dealt = [held([P, FP4_BYTES * ROWS], U8, f"w1_dealt{o}") for o in range(PASSES)]
         for o in range(PASSES):
-            deal_words(nc.vector, w1_dealt[o][:], w1_raw[:, 2 * ROWS * o : 2 * ROWS * (o + 1)])
-        picked = [held([P, PICKED], U32, "picked0")]
-        nc.vector.tensor_copy(picked[0][:], x_table[0][:].bitcast(U32).indirect(offs_list[:]))
-        w1_plane = [shared([P, ROWS], U8, "w1_plane0", "x_table0"), held([P, ROWS], U8, "w1_plane1")]
+            deal_words(w1_dealt[o][:], w1_raw[:, FP4_BYTES * ROWS * o : FP4_BYTES * ROWS * (o + 1)])
+        half = PACK // PASSES
+        picked = [held([P, PICKED], U32, f"picked{o}") for o in range(PASSES)]
+        w1_plane = []
         for o in range(PASSES):
-            deal_scales(nc.vector, w1_plane[o][:], w1_rows[:, o * ROWS : (o + 1) * ROWS])
-        picked.append(shared([P, PICKED], U32, "picked1", "w1_rows_picked1"))
-        nc.vector.tensor_copy(picked[1][:], x_table[1][:].bitcast(U32).indirect(offs_list[:]))
+            nc.vector.tensor_copy(picked[o][:], x_table[o][:].bitcast(U32).indirect(offs_list[:]))
+            plane = shared([P, PASSES, half * P], U8, f"w1_plane{o}", f"x_table{o}")
+            nc.vector.tensor_copy(
+                out=plane[:].rearrange("p o (t m) -> p o t m", t=half),
+                in_=w1_rows[:].rearrange("p (o m t) -> p o t m", o=PASSES, t=PACK)[:, :, half * o : half * (o + 1), :],
+            )
+            w1_plane.append(plane)
 
         y_banks = [psum.tile([P, BANK], F32, name="bank") for t in range(PACK)]
-        for o in range(PASSES):
-            for t in range(PACK):
+        for t in range(PACK):
+            for o in range(PASSES):
                 nc.tensor.matmul_mx(
                     out=y_banks[t][:],
-                    lhsT=w1_dealt[o][:, 2 * P * t : 2 * P * (t + 1)].bitcast(FP4X4),
-                    lhsT_scale=w1_plane[o][:, P * t : P * (t + 1)],
+                    lhsT=fp4_columns(w1_dealt[o], t),
+                    lhsT_scale=w1_plane[t // half][:, o, P * (t % half) : P * (t % half + 1)],
                     rhs=picked[o][:].bitcast(FP8X4),
                     rhs_scale=picked_plane[:, o * PICKED : (o + 1) * PICKED],
                     start=(o == 0),
                     stop=(o == PASSES - 1),
                 )
 
-        unit_cols = shared([P, PACK], F32, "unit_cols", "w1_raw_unit")
-        nc.sync.dma_start(out=unit_cols[:], in_=unit.rearrange("(p t) o -> p (t o)", t=PACK))
-        w2_raw = shared([P, 2 * ROWS], U8, "w2_raw", "picked_rows_w2_raw")
+        unit_cols = shared([P, PACK], F32, "unit_cols", "x_rows_unit")
+        nc.gpsimd.dma_start(out=unit_cols[:], in_=unit.rearrange("(p t) o -> p (t o)", t=PACK))
+        w2_raw = shared([P, FP4_BYTES * ROWS], U8, "w2_raw", "picked_rows_w2_raw")
         nc.sync.dma_start(out=w2_raw[:].bitcast(I32), in_=w2_words[0].bitcast(I32))
-        w2_rows = shared([P, ROWS], U8, "w2_rows", "x_table1")
+        w2_rows = shared([P, ROWS], U8, "w2_rows", "w1_raw_w2_rows")
         nc.gpsimd.memset(w2_rows[:].bitcast(I32), 0)
         load_scale_rows(nc.sync, w2_rows, w2_scales)
-        w2_dealt = held([P, 2 * ROWS], U8, "w2_dealt")
+        w2_dealt = held([P, FP4_BYTES * ROWS], U8, "w2_dealt")
         w2_plane = held([P, ROWS], U8, "w2_plane")
-        deal_words(nc.vector, w2_dealt[:], w2_raw[:])
+        deal_words(w2_dealt[:], w2_raw[:])
 
         y_plain = [held([P, PICKED], F32, f"y_plain{t}") for t in range(PACK)]
+        y_unit = [held([P, PICKED], F32, f"y_unit{t}") for t in range(PACK)]
         y_tanh = [held([P, PICKED], F32, f"y_tanh{t}") for t in range(PACK)]
         for t in range(PACK):
             nc.scalar.activation(y_tanh[t][:], y_banks[t][:], ACT.Tanh)
             nc.vector.tensor_copy(y_plain[t][:], y_banks[t][:])
-        deal_scales(nc.vector, w2_plane[:], w2_rows[:])
+            nc.vector.tensor_scalar(y_unit[t][:], y_plain[t][:], unit_cols[:, t : t + 1], None, ALU.mult)
+        nc.vector.tensor_copy(
+            out=w2_plane[:].rearrange("p (t m) -> p t m", t=PACK),
+            in_=w2_rows[:].rearrange("p (m t) -> p t m", t=PACK),
+        )
 
         out_rows = out_0.rearrange("(p t) r -> p t r", t=PACK)
         out_words = out_1[0].rearrange("p c r -> p (c r)").bitcast(I32)
         out_plane = held([P, TRIPLES], U8, "out_plane")
 
-        def weave(flat):
-            return flat.rearrange("p (c i t) -> p c t i", i=4, t=PACK)
+        def woven(flat):
+            return flat.rearrange("p (c i t) -> p c t i", i=LINE, t=PACK)
 
-        def rows(stack):
-            return stack.rearrange("p t (c i) -> p c t i", i=4)
+        def by_lines(stack):
+            return stack.rearrange("p t (c i) -> p c t i", i=LINE)
 
         def look_up(c, r0, n):
-            cols = slice(r0 // 16, (r0 + n) // 16)
-            third = held([P, PACK, n], F32, f"third{c}")
+            cols = slice(r0 // PER_COLUMN, (r0 + n) // PER_COLUMN)
+            third = shared([P, PACK, n], F32, f"third{c}", f"words_then_third{max(c, 1)}")
             summed = held([P, PACK, n], F32, f"summed{c}")
+            for t in range(PACK):
+                nc.scalar.activation(third[:, t, :], y_tanh[t][:].indirect(gc_list[:, cols]), ACT.Copy)
+                nc.vector.tensor_tensor(
+                    summed[:, t, :], y_plain[t][:].indirect(gb_list[:, cols]), third[:, t, :], ALU.add
+                )
             first = held([P, PACK, n], F32, f"first{c}")
             for t in range(PACK):
-                nc.scalar.activation(third[:, t, :], y_tanh[t][:].indirect(lists["c"][:, cols]), ACT.Copy)
-                nc.vector.tensor_tensor(
-                    summed[:, t, :], y_plain[t][:].indirect(lists["b"][:, cols]), third[:, t, :], ALU.add
-                )
-            return summed, first, cols
+                looked_up = y_unit[t][:].indirect(ga_list[:, cols])
+                if t >= PACK - GA_ON_VECTOR[c]:
+                    nc.vector.tensor_copy(first[:, t, :], looked_up)
+                else:
+                    nc.scalar.activation(first[:, t, :], looked_up, ACT.Copy)
+            return first, summed
 
-        def look_up_first(first, cols, ts):
-            for t in ts:
-                nc.scalar.activation(first[:, t, :], y_plain[t][:].indirect(lists["a"][:, cols]), ACT.Copy)
-
-        def multiply(c, n, summed, first):
+        def multiply(c, n, first, summed):
             hid = held([P, PACK * n], BF16, f"hid{c}")
-            exact = held([P, PACK, n], F32, f"exact{c}")
-            for t in range(PACK):
-                nc.vector.scalar_tensor_tensor(
-                    exact[:, t, :], first[:, t, :], unit_cols[:, t : t + 1], summed[:, t, :], ALU.mult, ALU.mult
-                )
-            nc.vector.tensor_copy(weave(hid[:]), rows(exact[:]))
-            hid_words = held([P, n], U32, f"hid_words{c}")
+            nc.vector.tensor_tensor(woven(hid[:]), by_lines(summed[:]), by_lines(first[:]), ALU.mult)
+            hid_words = shared([P, n], U32, f"hid_words{c}", f"words_then_third{c + 2}")
             hid_plane = held([P, n], U8, f"hid_plane{c}")
             nc.vector.quantize_mx(out=hid_words[:].bitcast(FP8X4), scales=hid_plane[:], in_=hid[:])
-            per_bank = BANK // n
-            banks = []
+            banks = [psum.tile([P, BANK], F32, name="bank") for b in range(PACK * n // BANK)]
             for t in range(PACK):
-                if t % per_bank == 0:
-                    banks.append(psum.tile([P, BANK], F32, name="bank"))
-                nc.tensor.matmul_mx(
-                    out=banks[-1][:, (t % per_bank) * n : (t % per_bank + 1) * n],
-                    lhsT=w2_dealt[:, 2 * P * t : 2 * P * (t + 1)].bitcast(FP4X4),
-                    lhsT_scale=w2_plane[:, P * t : P * (t + 1)],
-                    rhs=hid_words[:].bitcast(FP8X4),
-                    rhs_scale=hid_plane[:],
-                    start=True,
-                    stop=True,
-                )
+                done = 0
+                while done < n:
+                    place = t * n + done
+                    room = min(n - done, BANK - place % BANK)
+                    width = max(w for w in WIDTHS if w <= room)
+                    nc.tensor.matmul_mx(
+                        out=banks[place // BANK][:, place % BANK : place % BANK + width],
+                        lhsT=fp4_columns(w2_dealt, t),
+                        lhsT_scale=w2_plane[:, P * t : P * (t + 1)],
+                        rhs=hid_words[:, done : done + width].bitcast(FP8X4),
+                        rhs_scale=hid_plane[:, done : done + width],
+                        start=True,
+                        stop=True,
+                    )
+                    done += width
             return banks
 
         def hand_out(c, r0, n, banks):
             result = held([P, PACK, n], F32, f"result{c}")
             flat = result[:].rearrange("p t r -> p (t r)")
             for b, bank in enumerate(banks):
-                if PACK * r0 // BANK + b < VECTOR_EMPTIES:
-                    nc.vector.tensor_copy(flat[:, b * BANK : (b + 1) * BANK], bank[:])
-                else:
-                    nc.scalar.copy(flat[:, b * BANK : (b + 1) * BANK], bank[:])
+                nc.scalar.copy(flat[:, b * BANK : (b + 1) * BANK], bank[:])
             nc.sync.dma_start(out=out_rows[:, :, r0 : r0 + n], in_=result[:])
             rounded = held([P, PACK * n], BF16, f"rounded{c}")
-            nc.vector.tensor_copy(weave(rounded[:]), rows(result[:]))
+            nc.vector.tensor_copy(woven(rounded[:]), by_lines(result[:]))
             words = held([P, n], I32, f"words{c}")
             nc.vector.quantize_mx(out=words[:].bitcast(FP8X4), scales=out_plane[:, r0 : r0 + n], in_=rounded[:])
             nc.sync.dma_start(out=out_words[:, r0 : r0 + n], in_=words[:])
@@ -211,16 +228,16 @@ def tile_picked_ytripco_mul_po_kernel(
         pending = None
         r0 = 0
         for c, n in enumerate(CHUNKS):
-            summed, first, cols = look_up(c, r0, n)
-            look_up_first(first, cols, (0,))
+            first, summed = look_up(c, r0, n)
+            banks = multiply(c, n, first, summed)
             if pending is not None:
                 hand_out(*pending)
-            look_up_first(first, cols, (1, 2, 3))
-            pending = (c, r0, n, multiply(c, n, summed, first))
+            pending = (c, r0, n, banks)
             r0 += n
         hand_out(*pending)
-        for q in range(4):
+        for q in range(QUADS):
             queue = nc.scalar if q % 2 == 0 else nc.sync
             queue.dma_start(
-                out=out_2[0, 4 * q : 4 * q + 4, :].bitcast(I32), in_=out_plane[32 * q : 32 * q + 4, :].bitcast(I32)
+                out=out_2[0, LIVE * q : LIVE * (q + 1), :].bitcast(I32),
+                in_=out_plane[QUAD * q : QUAD * q + LIVE, :].bitcast(I32),
             )

from contextlib import ExitStack

import concourse.mybir as mybir

F32 = mybir.dt.float32
BF16 = mybir.dt.bfloat16
I32 = mybir.dt.int32
U32 = mybir.dt.uint32
U16 = mybir.dt.uint16
U8 = mybir.dt.uint8
FP8X4 = mybir.dt.float8_e4m3fn_x4
FP4X4 = mybir.dt.float4_e2m1fn_x4
ACT = mybir.ActivationFunctionType
ALU = mybir.AluOpType

P = 128
PACK = 4
QUADS = 4
QUAD = 32
LIVE = 4
PASSES = 2
GENES = 2048
PICKED = 512
ROWS = 512
TRIPLES = 1024
PER_COLUMN = 16
FP4_BYTES = 2
BANK = 512
BANKS = 8
LINE = 4
WIDTHS = (128, 256, 512)

CHUNKS = (384, 256, 256, 128)
GA_ON_VECTOR = (1, 2, 1, 1)

FLOPS = 2 * PASSES * PACK * P * ROWS * PICKED + 2 * ROWS * ROWS * TRIPLES


def tile_picked_ytripco_mul_po_kernel(
    tc, x_words, x_scales, w1_words, w1_scales, unit, w2_words, w2_scales, offs, ga, gb, gc, out_0, out_1, out_2
):
    nc = tc.nc
    with ExitStack() as ctx:
        keep = ctx.enter_context(tc.tile_pool(name="keep", bufs=1))
        psum = ctx.enter_context(tc.psum_pool(name="psum", bufs=BANKS))

        def held(shape, dtype, name):
            return keep.tile(shape, dtype, name=name, align_bytes=64)

        def shared(shape, dtype, name, tag):
            return keep.tile(shape, dtype, name=name, tag=tag, align_bytes=64)

        def load_scale_rows(queue, plane, scales):
            for q in range(QUADS):
                queue.dma_start(
                    out=plane[QUAD * q : QUAD * q + LIVE, :]
                    .bitcast(I32)
                    .rearrange("r (o c) -> r o c", o=scales.shape[0]),
                    in_=scales[:, LIVE * q : LIVE * (q + 1), :].bitcast(I32).rearrange("o r c -> r o c"),
                )

        def deal_words(dealt, raw):
            nc.vector.tensor_copy(
                out=dealt.rearrange("p (t m b) -> p t m b", t=PACK, b=FP4_BYTES),
                in_=raw.rearrange("p (m t b) -> p t m b", t=PACK, b=FP4_BYTES),
            )

        def fp4_columns(dealt, t):
            return dealt[:, FP4_BYTES * P * t : FP4_BYTES * P * (t + 1)].bitcast(FP4X4)

        rows_start = P - PASSES * QUADS * LIVE
        x_rows = shared([P, GENES], U8, "x_rows", "x_rows_unit")
        nc.sync.dma_start(
            out=x_rows[rows_start:, :].bitcast(I32), in_=x_scales.rearrange("o q c -> (o q) c").bitcast(I32)
        )
        nc.vector.memset(x_rows[:rows_start, :].bitcast(I32), 0)
        w1_rows = held([P, PASSES * ROWS], U8, "w1_rows")
        nc.gpsimd.memset(w1_rows[:].bitcast(I32), 0)
        picked_plane = held([P, PASSES * PICKED], U8, "picked_plane")
        nc.vector.memset(picked_plane[:].bitcast(I32), 0)

        offs_list = held([P, PICKED // PER_COLUMN], U16, "offs_list")
        nc.sync.dma_start(offs_list[:], offs)
        ga_list = held([P, TRIPLES // PER_COLUMN], U16, "ga_list")
        gb_list = held([P, TRIPLES // PER_COLUMN], U16, "gb_list")
        gc_list = held([P, TRIPLES // PER_COLUMN], U16, "gc_list")
        nc.sync.dma_start(gc_list[:], gc)
        nc.sync.dma_start(gb_list[:], gb)
        nc.sync.dma_start(ga_list[:], ga)
        w1_raw = shared([P, PASSES * FP4_BYTES * ROWS], U8, "w1_raw", "w1_raw_w2_rows")
        nc.sync.dma_start(
            out=w1_raw[:].bitcast(I32).rearrange("p (o c) -> p o c", o=PASSES),
            in_=w1_words.bitcast(I32).rearrange("o p c -> p o c"),
        )
        x_table = []
        for o in range(PASSES):
            table = shared([P, GENES], I32, f"x_table{o}", f"x_table{o}")
            nc.sync.dma_start(out=table[:], in_=x_words[o].rearrange("p c r -> p (c r)").bitcast(I32))
            x_table.append(table)
        load_scale_rows(nc.gpsimd, w1_rows, w1_scales)

        picked_rows = shared([P, PICKED], U8, "picked_rows", "picked_rows_w2_raw")
        nc.vector.tensor_copy(picked_rows[:], x_rows[:].indirect(offs_list[:]))
        for o in range(PASSES):
            for q in range(QUADS):
                queue = nc.gpsimd if (o, q) == (PASSES - 1, QUADS - 1) else nc.scalar
                row = rows_start + LIVE * (QUADS * o + q)
                queue.dma_start(
                    out=picked_plane[QUAD * q : QUAD * q + LIVE, o * PICKED : (o + 1) * PICKED].bitcast(I32),
                    in_=picked_rows[row : row + LIVE, :].bitcast(I32),
                )
        w1_dealt = [held([P, FP4_BYTES * ROWS], U8, f"w1_dealt{o}") for o in range(PASSES)]
        for o in range(PASSES):
            deal_words(w1_dealt[o][:], w1_raw[:, FP4_BYTES * ROWS * o : FP4_BYTES * ROWS * (o + 1)])
        half = PACK // PASSES
        picked = [held([P, PICKED], U32, f"picked{o}") for o in range(PASSES)]
        w1_plane = []
        for o in range(PASSES):
            nc.vector.tensor_copy(picked[o][:], x_table[o][:].bitcast(U32).indirect(offs_list[:]))
            plane = shared([P, PASSES, half * P], U8, f"w1_plane{o}", f"x_table{o}")
            nc.vector.tensor_copy(
                out=plane[:].rearrange("p o (t m) -> p o t m", t=half),
                in_=w1_rows[:].rearrange("p (o m t) -> p o t m", o=PASSES, t=PACK)[:, :, half * o : half * (o + 1), :],
            )
            w1_plane.append(plane)

        y_banks = [psum.tile([P, BANK], F32, name="bank") for t in range(PACK)]
        for t in range(PACK):
            for o in range(PASSES):
                nc.tensor.matmul_mx(
                    out=y_banks[t][:],
                    lhsT=fp4_columns(w1_dealt[o], t),
                    lhsT_scale=w1_plane[t // half][:, o, P * (t % half) : P * (t % half + 1)],
                    rhs=picked[o][:].bitcast(FP8X4),
                    rhs_scale=picked_plane[:, o * PICKED : (o + 1) * PICKED],
                    start=(o == 0),
                    stop=(o == PASSES - 1),
                )

        unit_cols = shared([P, PACK], F32, "unit_cols", "x_rows_unit")
        nc.gpsimd.dma_start(out=unit_cols[:], in_=unit.rearrange("(p t) o -> p (t o)", t=PACK))
        w2_raw = shared([P, FP4_BYTES * ROWS], U8, "w2_raw", "picked_rows_w2_raw")
        nc.sync.dma_start(out=w2_raw[:].bitcast(I32), in_=w2_words[0].bitcast(I32))
        w2_rows = shared([P, ROWS], U8, "w2_rows", "w1_raw_w2_rows")
        nc.gpsimd.memset(w2_rows[:].bitcast(I32), 0)
        load_scale_rows(nc.sync, w2_rows, w2_scales)
        w2_dealt = held([P, FP4_BYTES * ROWS], U8, "w2_dealt")
        w2_plane = held([P, ROWS], U8, "w2_plane")
        deal_words(w2_dealt[:], w2_raw[:])

        y_plain = [held([P, PICKED], F32, f"y_plain{t}") for t in range(PACK)]
        y_unit = [held([P, PICKED], F32, f"y_unit{t}") for t in range(PACK)]
        y_tanh = [held([P, PICKED], F32, f"y_tanh{t}") for t in range(PACK)]
        for t in range(PACK):
            nc.scalar.activation(y_tanh[t][:], y_banks[t][:], ACT.Tanh)
            nc.vector.tensor_copy(y_plain[t][:], y_banks[t][:])
            nc.vector.tensor_scalar(y_unit[t][:], y_plain[t][:], unit_cols[:, t : t + 1], None, ALU.mult)
        nc.vector.tensor_copy(
            out=w2_plane[:].rearrange("p (t m) -> p t m", t=PACK),
            in_=w2_rows[:].rearrange("p (m t) -> p t m", t=PACK),
        )

        out_rows = out_0.rearrange("(p t) r -> p t r", t=PACK)
        out_words = out_1[0].rearrange("p c r -> p (c r)").bitcast(I32)
        out_plane = held([P, TRIPLES], U8, "out_plane")

        def woven(flat):
            return flat.rearrange("p (c i t) -> p c t i", i=LINE, t=PACK)

        def by_lines(stack):
            return stack.rearrange("p t (c i) -> p c t i", i=LINE)

        def look_up(c, r0, n):
            cols = slice(r0 // PER_COLUMN, (r0 + n) // PER_COLUMN)
            third = shared([P, PACK, n], F32, f"third{c}", f"words_then_third{max(c, 1)}")
            summed = held([P, PACK, n], F32, f"summed{c}")
            for t in range(PACK):
                nc.scalar.activation(third[:, t, :], y_tanh[t][:].indirect(gc_list[:, cols]), ACT.Copy)
                nc.vector.tensor_tensor(
                    summed[:, t, :], y_plain[t][:].indirect(gb_list[:, cols]), third[:, t, :], ALU.add
                )
            first = held([P, PACK, n], F32, f"first{c}")
            for t in range(PACK):
                looked_up = y_unit[t][:].indirect(ga_list[:, cols])
                if t >= PACK - GA_ON_VECTOR[c]:
                    nc.vector.tensor_copy(first[:, t, :], looked_up)
                else:
                    nc.scalar.activation(first[:, t, :], looked_up, ACT.Copy)
            return first, summed

        def multiply(c, n, first, summed):
            hid = held([P, PACK * n], BF16, f"hid{c}")
            nc.vector.tensor_tensor(woven(hid[:]), by_lines(summed[:]), by_lines(first[:]), ALU.mult)
            hid_words = shared([P, n], U32, f"hid_words{c}", f"words_then_third{c + 2}")
            hid_plane = held([P, n], U8, f"hid_plane{c}")
            nc.vector.quantize_mx(out=hid_words[:].bitcast(FP8X4), scales=hid_plane[:], in_=hid[:])
            banks = [psum.tile([P, BANK], F32, name="bank") for b in range(PACK * n // BANK)]
            for t in range(PACK):
                done = 0
                while done < n:
                    place = t * n + done
                    room = min(n - done, BANK - place % BANK)
                    width = max(w for w in WIDTHS if w <= room)
                    nc.tensor.matmul_mx(
                        out=banks[place // BANK][:, place % BANK : place % BANK + width],
                        lhsT=fp4_columns(w2_dealt, t),
                        lhsT_scale=w2_plane[:, P * t : P * (t + 1)],
                        rhs=hid_words[:, done : done + width].bitcast(FP8X4),
                        rhs_scale=hid_plane[:, done : done + width],
                        start=True,
                        stop=True,
                    )
                    done += width
            return banks

        def hand_out(c, r0, n, banks):
            result = held([P, PACK, n], F32, f"result{c}")
            flat = result[:].rearrange("p t r -> p (t r)")
            for b, bank in enumerate(banks):
                nc.scalar.copy(flat[:, b * BANK : (b + 1) * BANK], bank[:])
            nc.sync.dma_start(out=out_rows[:, :, r0 : r0 + n], in_=result[:])
            rounded = held([P, PACK * n], BF16, f"rounded{c}")
            nc.vector.tensor_copy(woven(rounded[:]), by_lines(result[:]))
            words = held([P, n], I32, f"words{c}")
            nc.vector.quantize_mx(out=words[:].bitcast(FP8X4), scales=out_plane[:, r0 : r0 + n], in_=rounded[:])
            nc.sync.dma_start(out=out_words[:, r0 : r0 + n], in_=words[:])

        pending = None
        r0 = 0
        for c, n in enumerate(CHUNKS):
            first, summed = look_up(c, r0, n)
            banks = multiply(c, n, first, summed)
            if pending is not None:
                hand_out(*pending)
            pending = (c, r0, n, banks)
            r0 += n
        hand_out(*pending)
        for q in range(QUADS):
            queue = nc.scalar if q % 2 == 0 else nc.sync
            queue.dma_start(
                out=out_2[0, LIVE * q : LIVE * (q + 1), :].bitcast(I32),
                in_=out_plane[QUAD * q : QUAD * q + LIVE, :].bitcast(I32),
            )
